import numpy as np
import ml_dtypes

BF16 = ml_dtypes.bfloat16


def bf(x):
    return np.asarray(x, np.float32).astype(BF16)


def f32(x):
    return np.asarray(x, np.float32)


def f64(x):
    return np.asarray(x).astype(np.float64)


def striped(idx):
    return np.tile(idx.reshape(-1, 16).T, (8, 1))


A, S, K, M, N, E, Q = 256, 512, 128, 512, 512, 2, 256


def setup_inputs():
    return {"a": bf(np.random.standard_normal((A, S))), "wd": bf(np.random.standard_normal((A, M)) / np.sqrt(A)), "x": bf(np.random.standard_normal((K, N))), "w": bf(1.2 * np.random.standard_normal((E, K, M)) / np.sqrt(K)), "s": f32(0.5 + np.random.random_sample((M, 1))), "offs": striped(np.random.permutation(S))}


def reference(a, wd, x, w, s, offs):
    idx = offs[:16].T.reshape(-1)
    z = f64(wd).T @ f64(a)
    for e in range(E):
        z[:, idx[e * Q : (e + 1) * Q]] += f64(w)[e].T @ f64(x)[:, e * Q : (e + 1) * Q]
    z = z / np.sqrt((z**2).mean(axis=0, keepdims=True) + 1e-5) * f64(s)
    return z

@@ -1,0 +1,81 @@
+import concourse.mybir as mybir
+
+P = 128
+D, S, K, M, E, Q = 256, 512, 128, 512, 2, 256
+DC = D // P
+MB = M // P
+EPS = 1e-5
+
+FLOPS = 2 * M * D * S + 2 * M * K * S + 4 * M * S
+
+BF16, F32, U16 = mybir.dt.bfloat16, mybir.dt.float32, mybir.dt.uint16
+MULT = mybir.AluOpType.mult
+ACT = mybir.ActivationFunctionType
+
+
+def tile_rows_placenorm_proj_kernel(tc, a, wd, x, w, s, offs, out):
+    nc = tc.nc
+    with (
+        tc.tile_pool(name="held", bufs=1) as held,
+        tc.tile_pool(name="work", bufs=MB) as work,
+        tc.psum_pool(name="psum", bufs=1) as psum,
+    ):
+        a_sb = held.tile([P, DC, S], BF16)
+        nc.sync.dma_start(a_sb[:], a.rearrange("(p c) i -> p c i", c=DC))
+        wd_sb = held.tile([P, DC, M], BF16)
+        nc.scalar.dma_start(wd_sb[:], wd.rearrange("(p c) m -> p c m", c=DC))
+        x_sb = held.tile([P, S], BF16)
+        nc.sync.dma_start(x_sb[:], x)
+        w_sb = held.tile([P, E, M], BF16)
+        nc.scalar.dma_start(w_sb[:], w.rearrange("e k m -> k e m"))
+        offsets = held.tile([P, S // 16], U16)
+        nc.sync.dma_start(offsets[:], offs)
+        gain = held.tile([P, MB], F32)
+        nc.scalar.dma_start(gain[:], s.rearrange("(b p) o -> p (b o)", p=P))
+
+        eps = held.tile([P, 1], F32)
+        nc.vector.memset(eps[:], EPS)
+        mean_weights = held.tile([P, P], BF16)
+        nc.vector.memset(mean_weights[:], 1.0 / M)
+        table_load = held.tile([P, 1], F32)
+        nc.scalar.activation(table_load[:], eps[:], ACT.Abs_reciprocal_sqrt, bias=eps[:])
+
+        windows = [psum.tile([P, S], F32, name=f"window{b}") for b in range(MB)]
+        for b in range(MB):
+            for c in range(DC):
+                nc.tensor.matmul(
+                    windows[b][:],
+                    wd_sb[:, c, b * P : (b + 1) * P],
+                    a_sb[:, c, :],
+                    start=(c == 0),
+                    stop=False,
+                )
+
+        for b in range(MB):
+            for e in range(E):
+                places = offsets[:, e * Q // 16 : (e + 1) * Q // 16]
+                nc.tensor.matmul(
+                    windows[b][:].indirect(places),
+                    w_sb[:, e, b * P : (b + 1) * P],
+                    x_sb[:, e * Q : (e + 1) * Q],
+                    start=False,
+                    stop=(e == E - 1),
+                )
+
+        mean = psum.tile([P, S], F32)
+        for b in range(MB):
+            squares = work.tile([P, S], BF16)
+            nc.scalar.activation(squares[:], windows[b][:], ACT.Square)
+            nc.tensor.matmul(
+                mean[:], mean_weights[:], squares[:], start=(b == 0), stop=(b == MB - 1)
+            )
+        rstd = held.tile([P, S], F32)
+        nc.scalar.activation(rstd[:], mean[:], ACT.Abs_reciprocal_sqrt, bias=eps[:])
+
+        out_blocks = out.rearrange("(b p) i -> b p i", p=P)
+        for b in range(MB):
+            normed = work.tile([P, S], F32)
+            nc.vector.scalar_tensor_tensor(
+                normed[:], windows[b][:], gain[:, b : b + 1], rstd[:], MULT, MULT
+            )
+            nc.sync.dma_start(out_blocks[b], normed[:])

@@ -4,7 +4,9 @@ P = 128
 D, S, K, M, E, Q = 256, 512, 128, 512, 2, 256
 DC = D // P
 MB = M // P
+H = S // 2
 EPS = 1e-5
+WARM_UPS = 3
 
 FLOPS = 2 * M * D * S + 2 * M * K * S + 4 * M * S
 
@@ -17,13 +19,16 @@ def tile_rows_placenorm_proj_kernel(tc, a, wd, x, w, s, offs, out):
     nc = tc.nc
     with (
         tc.tile_pool(name="held", bufs=1) as held,
-        tc.tile_pool(name="work", bufs=MB) as work,
+        tc.tile_pool(name="work", bufs=2 * MB) as work,
         tc.psum_pool(name="psum", bufs=1) as psum,
     ):
-        a_sb = held.tile([P, DC, S], BF16)
-        nc.sync.dma_start(a_sb[:], a.rearrange("(p c) i -> p c i", c=DC))
-        wd_sb = held.tile([P, DC, M], BF16)
-        nc.scalar.dma_start(wd_sb[:], wd.rearrange("(p c) m -> p c m", c=DC))
+        a_blocks = a.rearrange("(c p) i -> c p i", p=P)
+        wd_blocks = wd.rearrange("(c p) m -> c p m", p=P)
+        a_sb = [held.tile([P, S], BF16, name=f"a{c}") for c in range(DC)]
+        wd_sb = [held.tile([P, M], BF16, name=f"wd{c}") for c in range(DC)]
+        for c in range(DC):
+            nc.sync.dma_start(a_sb[c][:], a_blocks[c])
+            nc.scalar.dma_start(wd_sb[c][:], wd_blocks[c])
         x_sb = held.tile([P, S], BF16)
         nc.sync.dma_start(x_sb[:], x)
         w_sb = held.tile([P, E, M], BF16)
@@ -33,6 +38,8 @@ def tile_rows_placenorm_proj_kernel(tc, a, wd, x, w, s, offs, out):
         gain = held.tile([P, MB], F32)
         nc.scalar.dma_start(gain[:], s.rearrange("(b p) o -> p (b o)", p=P))
 
+        zeros = held.tile([P, S], BF16)
+        nc.vector.memset(zeros[:], 0.0)
         eps = held.tile([P, 1], F32)
         nc.vector.memset(eps[:], EPS)
         mean_weights = held.tile([P, P], BF16)
@@ -40,13 +47,17 @@ def tile_rows_placenorm_proj_kernel(tc, a, wd, x, w, s, offs, out):
         table_load = held.tile([P, 1], F32)
         nc.scalar.activation(table_load[:], eps[:], ACT.Abs_reciprocal_sqrt, bias=eps[:])
 
+        spare = psum.tile([P, S], F32)
+        for i in range(WARM_UPS):
+            nc.tensor.matmul(spare[:], zeros[:, :P], zeros[:], start=True, stop=True)
+
         windows = [psum.tile([P, S], F32, name=f"window{b}") for b in range(MB)]
-        for b in range(MB):
-            for c in range(DC):
+        for c in range(DC):
+            for b in range(MB):
                 nc.tensor.matmul(
                     windows[b][:],
-                    wd_sb[:, c, b * P : (b + 1) * P],
-                    a_sb[:, c, :],
+                    wd_sb[c][:, b * P : (b + 1) * P],
+                    a_sb[c][:],
                     start=(c == 0),
                     stop=False,
                 )
@@ -62,20 +73,32 @@ def tile_rows_placenorm_proj_kernel(tc, a, wd, x, w, s, offs, out):
                     stop=(e == E - 1),
                 )
 
-        mean = psum.tile([P, S], F32)
-        for b in range(MB):
-            squares = work.tile([P, S], BF16)
-            nc.scalar.activation(squares[:], windows[b][:], ACT.Square)
-            nc.tensor.matmul(
-                mean[:], mean_weights[:], squares[:], start=(b == 0), stop=(b == MB - 1)
-            )
-        rstd = held.tile([P, S], F32)
-        nc.scalar.activation(rstd[:], mean[:], ACT.Abs_reciprocal_sqrt, bias=eps[:])
-
         out_blocks = out.rearrange("(b p) i -> b p i", p=P)
-        for b in range(MB):
-            normed = work.tile([P, S], F32)
-            nc.vector.scalar_tensor_tensor(
-                normed[:], windows[b][:], gain[:, b : b + 1], rstd[:], MULT, MULT
+        means = [psum.tile([P, H], F32, name=f"mean{h}") for h in range(2)]
+        rstd = held.tile([P, S], F32)
+        squares = [held.tile([P, S], BF16, name=f"squares{b}") for b in range(MB)]
+        for b in range(MB - 1):
+            nc.scalar.activation(squares[b][:], windows[b][:], ACT.Square)
+        halves = [slice(h * H, (h + 1) * H) for h in range(2)]
+        for cols in halves:
+            nc.scalar.activation(squares[MB - 1][:, cols], windows[MB - 1][:, cols], ACT.Square)
+        for h, cols in enumerate(halves):
+            for b in range(MB):
+                nc.tensor.matmul(
+                    means[h][:],
+                    mean_weights[:],
+                    squares[b][:, cols],
+                    start=(b == 0),
+                    stop=(b == MB - 1),
+                )
+            nc.scalar.activation(
+                rstd[:, cols], means[h][:], ACT.Abs_reciprocal_sqrt, bias=eps[:]
             )
-            nc.sync.dma_start(out_blocks[b], normed[:])
+
+        for cols in halves:
+            for b in range(MB):
+                normed = work.tile([P, H], F32)
+                nc.vector.scalar_tensor_tensor(
+                    normed[:], windows[b][:, cols], gain[:, b : b + 1], rstd[:, cols], MULT, MULT
+                )
+                nc.sync.dma_start(out_blocks[b][:, cols], normed[:])

@@ -28,15 +28,15 @@ def tile_rows_placenorm_proj_kernel(tc, a, wd, x, w, s, offs, out):
         wd_sb = [held.tile([P, M], BF16, name=f"wd{c}") for c in range(DC)]
         for c in range(DC):
             nc.sync.dma_start(a_sb[c][:], a_blocks[c])
-            nc.scalar.dma_start(wd_sb[c][:], wd_blocks[c])
+            nc.sync.dma_start(wd_sb[c][:], wd_blocks[c])
         x_sb = held.tile([P, S], BF16)
         nc.sync.dma_start(x_sb[:], x)
         w_sb = held.tile([P, E, M], BF16)
-        nc.scalar.dma_start(w_sb[:], w.rearrange("e k m -> k e m"))
+        nc.sync.dma_start(w_sb[:], w.rearrange("e k m -> k e m"))
         offsets = held.tile([P, S // 16], U16)
         nc.sync.dma_start(offsets[:], offs)
         gain = held.tile([P, MB], F32)
-        nc.scalar.dma_start(gain[:], s.rearrange("(b p) o -> p (b o)", p=P))
+        nc.sync.dma_start(gain[:], s.rearrange("(b p) o -> p (b o)", p=P))
 
         zeros = held.tile([P, S], BF16)
         nc.vector.memset(zeros[:], 0.0)

import concourse.mybir as mybir

P = 128
D, S, K, M, E, Q = 256, 512, 128, 512, 2, 256
DC = D // P
MB = M // P
H = S // 2
EPS = 1e-5
WARM_UPS = 3

FLOPS = 2 * M * D * S + 2 * M * K * S + 4 * M * S

BF16, F32, U16 = mybir.dt.bfloat16, mybir.dt.float32, mybir.dt.uint16
MULT = mybir.AluOpType.mult
ACT = mybir.ActivationFunctionType


def tile_rows_placenorm_proj_kernel(tc, a, wd, x, w, s, offs, out):
    nc = tc.nc
    with (
        tc.tile_pool(name="held", bufs=1) as held,
        tc.tile_pool(name="work", bufs=2 * MB) as work,
        tc.psum_pool(name="psum", bufs=1) as psum,
    ):
        a_blocks = a.rearrange("(c p) i -> c p i", p=P)
        wd_blocks = wd.rearrange("(c p) m -> c p m", p=P)
        a_sb = [held.tile([P, S], BF16, name=f"a{c}") for c in range(DC)]
        wd_sb = [held.tile([P, M], BF16, name=f"wd{c}") for c in range(DC)]
        for c in range(DC):
            nc.sync.dma_start(a_sb[c][:], a_blocks[c])
            nc.sync.dma_start(wd_sb[c][:], wd_blocks[c])
        x_sb = held.tile([P, S], BF16)
        nc.sync.dma_start(x_sb[:], x)
        w_sb = held.tile([P, E, M], BF16)
        nc.sync.dma_start(w_sb[:], w.rearrange("e k m -> k e m"))
        offsets = held.tile([P, S // 16], U16)
        nc.sync.dma_start(offsets[:], offs)
        gain = held.tile([P, MB], F32)
        nc.sync.dma_start(gain[:], s.rearrange("(b p) o -> p (b o)", p=P))

        zeros = held.tile([P, S], BF16)
        nc.vector.memset(zeros[:], 0.0)
        eps = held.tile([P, 1], F32)
        nc.vector.memset(eps[:], EPS)
        mean_weights = held.tile([P, P], BF16)
        nc.vector.memset(mean_weights[:], 1.0 / M)
        table_load = held.tile([P, 1], F32)
        nc.scalar.activation(table_load[:], eps[:], ACT.Abs_reciprocal_sqrt, bias=eps[:])

        spare = psum.tile([P, S], F32)
        for i in range(WARM_UPS):
            nc.tensor.matmul(spare[:], zeros[:, :P], zeros[:], start=True, stop=True)

        windows = [psum.tile([P, S], F32, name=f"window{b}") for b in range(MB)]
        for c in range(DC):
            for b in range(MB):
                nc.tensor.matmul(
                    windows[b][:],
                    wd_sb[c][:, b * P : (b + 1) * P],
                    a_sb[c][:],
                    start=(c == 0),
                    stop=False,
                )

        for b in range(MB):
            for e in range(E):
                places = offsets[:, e * Q // 16 : (e + 1) * Q // 16]
                nc.tensor.matmul(
                    windows[b][:].indirect(places),
                    w_sb[:, e, b * P : (b + 1) * P],
                    x_sb[:, e * Q : (e + 1) * Q],
                    start=False,
                    stop=(e == E - 1),
                )

        out_blocks = out.rearrange("(b p) i -> b p i", p=P)
        means = [psum.tile([P, H], F32, name=f"mean{h}") for h in range(2)]
        rstd = held.tile([P, S], F32)
        squares = [held.tile([P, S], BF16, name=f"squares{b}") for b in range(MB)]
        for b in range(MB - 1):
            nc.scalar.activation(squares[b][:], windows[b][:], ACT.Square)
        halves = [slice(h * H, (h + 1) * H) for h in range(2)]
        for cols in halves:
            nc.scalar.activation(squares[MB - 1][:, cols], windows[MB - 1][:, cols], ACT.Square)
        for h, cols in enumerate(halves):
            for b in range(MB):
                nc.tensor.matmul(
                    means[h][:],
                    mean_weights[:],
                    squares[b][:, cols],
                    start=(b == 0),
                    stop=(b == MB - 1),
                )
            nc.scalar.activation(
                rstd[:, cols], means[h][:], ACT.Abs_reciprocal_sqrt, bias=eps[:]
            )

        for cols in halves:
            for b in range(MB):
                normed = work.tile([P, H], F32)
                nc.vector.scalar_tensor_tensor(
                    normed[:], windows[b][:, cols], gain[:, b : b + 1], rstd[:, cols], MULT, MULT
                )
                nc.sync.dma_start(out_blocks[b][:, cols], normed[:])
